import numpy as np
import ml_dtypes


def mxq(x, axis, fmt="e4m3"):
    dtype, down = {"e4m3": (ml_dtypes.float8_e4m3fn, 7), "e5m2": (ml_dtypes.float8_e5m2, 14)}[fmt]
    v = np.moveaxis(np.asarray(x, np.float32).astype(ml_dtypes.bfloat16).astype(np.float64), axis, -1)
    blocks = v.reshape(v.shape[:-1] + (-1, 32))
    amax = np.abs(blocks).max(-1, keepdims=True)
    byte = np.maximum(np.where(amax > 0, np.frexp(amax)[1] - 1 + 127, 0) - down, 1)
    scale = np.exp2(byte - 127.0)
    codes = (blocks / scale).astype(np.float32).astype(dtype).astype(np.float64)
    return np.moveaxis((codes * scale).reshape(v.shape), -1, axis)


WIDE = False


def mx_kscale(k):
    if not WIDE:
        return np.ones(k)
    levels = np.array([10, -10, 5, -5, 0])
    if k % 512:
        return np.exp2(np.random.permutation(np.resize(levels, k // 32))).repeat(32)
    a = np.empty((k // 512, 16))
    for p in range(k // 512):
        a[p, :8] = np.random.permutation(np.resize(levels, 8))
        for g in range(8):
            far = levels[np.abs(levels - a[p, g]) >= 10]
            a[p, g + 8] = far[np.random.randint(len(far))]
    return np.exp2(a.ravel()).repeat(32)


def f64(x):
    return np.asarray(x).astype(np.float64)


def striped(idx):
    return np.tile(idx.reshape(-1, 16).T, (8, 1)).astype(np.uint16)


def unstriped(offs):
    return offs[:16].T.reshape(-1).astype(np.int64)


E2M1 = np.array([0.0, 0.5, 1.0, 1.5, 2.0, 3.0, 4.0, 6.0, -0.0, -0.5, -1.0, -1.5, -2.0, -3.0, -4.0, -6.0])


def pack_weight(w, fmt):
    k, n = w.shape
    w = f64(np.asarray(w, np.float32).astype(ml_dtypes.bfloat16)).reshape(k // 32, 32, n)
    amax = np.abs(w).max(1)
    if fmt == "e4m3":
        byte = np.frexp(amax)[1] - 1 + 127 - 7
    else:
        mant, ex = np.frexp(amax / 6.0)
        byte = np.where(mant > 0.5, ex, ex - 1) + 127
    byte = np.clip(np.where(amax > 0, byte, 1), 1, 254)
    scaled = (w * np.exp2(127.0 - byte)[:, None, :]).reshape(k, n).astype(np.float32)
    by_word = np.ascontiguousarray(scaled.reshape(k // 512, 128, 4, n).transpose(0, 1, 3, 2))
    if fmt == "e4m3":
        words = by_word.astype(ml_dtypes.float8_e4m3fn).view(np.uint8)
    else:
        c = by_word.astype(ml_dtypes.float4_e2m1fn).view(np.uint8) & 0xF
        words = (c[..., 0::2] | (c[..., 1::2] << 4)).reshape(k // 512, 128, 2 * n)
    return np.ascontiguousarray(words), np.ascontiguousarray(byte.astype(np.uint8).reshape(k // 512, 16, n))


def unpack_weight(words, scales, fmt):
    g, _, n = scales.shape
    words = np.ascontiguousarray(words).reshape(g, 128, n, -1)
    if fmt == "e4m3":
        vals = words.view(ml_dtypes.float8_e4m3fn).astype(np.float64)
    else:
        nib = np.empty((g, 128, n, 4), np.uint8)
        nib[..., 0::2] = words & 0xF
        nib[..., 1::2] = words >> 4
        vals = E2M1[nib]
    vals = vals * np.repeat(np.exp2(scales.astype(np.float64) - 127.0), 8, axis=1)[..., None]
    return vals.transpose(0, 1, 3, 2).reshape(g * 512, n)


def relu2(v):
    return np.maximum(v, 0.0) ** 2


K, T, E, C, H, N, TOP = 512, 512, 12, 128, 512, 512, 3


def by_expert(wq, xq):
    return np.concatenate([wq[e].T @ xq[:, e * C:(e + 1) * C] for e in range(E)], axis=1)


def setup_inputs():
    n = np.random.standard_normal
    s = mx_kscale(K)
    u = mx_kscale(H)
    deal = np.repeat(np.arange(E), C).reshape(TOP, T)[:, np.random.permutation(T)]
    deal = np.take_along_axis(deal, np.argsort(np.random.rand(TOP, T), axis=0), axis=0)
    for _ in range(8):
        s_, t_ = np.random.permutation(T).reshape(2, -1); r = np.random.randint(TOP, size=T // 2); x, y = deal[r, s_].copy(), deal[r, t_].copy()
        ok = ~((deal[:, s_] == y).any(0) | (deal[:, t_] == x).any(0)); deal[r[ok], s_[ok]] = y[ok]; deal[r[ok], t_[ok]] = x[ok]
    order = np.lexsort((np.random.rand(TOP * T), deal.reshape(-1)))
    slot_token = order % T; pos = np.empty(TOP * T, np.int64); pos[order] = np.arange(TOP * T); pos = pos.reshape(TOP, T)
    g = np.random.uniform(0.5, 1.5, (TOP, T)); g = g / g.sum(0)
    partner = np.concatenate([np.random.permutation(T) for _ in range(-(-E * C // T))])[:E * C]
    x = pack_weight(n((K, T)) * s[:, None], "e4m3")
    w1 = [pack_weight(m, "e2m1") for m in n((E, K, H)) / np.sqrt(K) / s[None, :, None] * u]
    wp = [pack_weight(m, "e2m1") for m in n((E, K, H)) / np.sqrt(K) / s[None, :, None] * u]
    w2 = [pack_weight(m, "e2m1") for m in n((E, H, N)) / np.sqrt(H) / u[None, :, None] ** 2]
    return {
        "x_words": x[0],
        "x_scales": x[1],
        "w1_words": np.stack([m[0] for m in w1]),
        "w1_scales": np.stack([m[1] for m in w1]),
        "wp_words": np.stack([m[0] for m in wp]),
        "wp_scales": np.stack([m[1] for m in wp]),
        "w2_words": np.stack([m[0] for m in w2]),
        "w2_scales": np.stack([m[1] for m in w2]),
        "gate": np.stack([np.tile(r, (128, 1)) for r in g]).astype(np.float32),
        "offs": striped(slot_token),
        "pos1": striped(pos[0]),
        "pos2": striped(pos[1]),
        "pos3": striped(pos[2]),
        "offs2": striped(partner),
    }


def reference(x_words, x_scales, w1_words, w1_scales, wp_words, wp_scales, w2_words, w2_scales, gate, offs, pos1, pos2, pos3, offs2):
    w1 = np.stack([unpack_weight(w1_words[e], w1_scales[e], "e2m1") for e in range(E)])
    wp = np.stack([unpack_weight(wp_words[e], wp_scales[e], "e2m1") for e in range(E)])
    w2 = np.stack([unpack_weight(w2_words[e], w2_scales[e], "e2m1") for e in range(E)])
    idx, idx2 = unstriped(offs), unstriped(offs2)
    x = unpack_weight(x_words, x_scales, "e4m3")
    h = relu2(by_expert(w1, x[:, idx]) + by_expert(wp, x[:, idx2]))
    y = by_expert(w2, mxq(h, 0, "e4m3"))
    out = sum(f64(gate[r, :1]) * y[:, unstriped(p)] for r, p in enumerate((pos1, pos2, pos3)))
    return out

@@ -1,0 +1,224 @@
+from contextlib import ExitStack
+
+import concourse.mybir as mybir
+from concourse.masks import make_identity
+
+K, T, E, C, H, N, TOP = 512, 512, 12, 128, 512, 512, 3
+S = E * C
+FLOPS = 2 * S * (2 * K * H + H * N)
+
+F32 = mybir.dt.float32
+BF16 = mybir.dt.bfloat16
+I32 = mybir.dt.int32
+U32 = mybir.dt.uint32
+U16 = mybir.dt.uint16
+U8 = mybir.dt.uint8
+FP8X4 = mybir.dt.float8_e4m3fn_x4
+FP4X4 = mybir.dt.float4_e2m1fn_x4
+ACT = mybir.ActivationFunctionType
+ALU = mybir.AluOpType
+
+P = 128
+NB = N // P
+GATHER_GROUPS = (1, 2, 2, 2, 2, 2, 1)
+GATHER_SLOTS = 2
+LOAD_GROUPS = (1, 1, 2, 2, 3, 3)
+LOAD_SLOTS = 3
+QUANT_GROUPS = (8, 2, 1, 1)
+
+
+def spans(sizes):
+    return [(sum(sizes[:g]), sum(sizes[: g + 1])) for g in range(len(sizes))]
+
+
+def tile_moe_duo_relu2_kernel(
+    tc, x_words, x_scales, w1_words, w1_scales, wp_words, wp_scales, w2_words, w2_scales,
+    gate, offs, pos1, pos2, pos3, offs2, out,
+):
+    nc = tc.nc
+    with ExitStack() as ctx:
+        keep = ctx.enter_context(tc.tile_pool(name="keep", bufs=1))
+        ring = ctx.enter_context(tc.tile_pool(name="ring", bufs=3))
+        psum = ctx.enter_context(tc.psum_pool(name="psum", bufs=1))
+
+        def bank(b, shape):
+            return psum.tile(shape, F32, name="bank%d" % b)
+
+        def load_list(name, src):
+            t = keep.tile([P, src.shape[1]], U16, name=name)
+            nc.sync.dma_start(t[:], src)
+            return t
+
+        def zeroed_plane(name, shape):
+            t = keep.tile(shape, U8, name=name, align_bytes=64)
+            nc.vector.memset(t[:].bitcast(I32), 0)
+            return t
+
+        def load_plane(plane, src):
+            rows = src[:, 0].rearrange("e (Q r) n -> r Q e n", r=4)
+            for r in range(4):
+                nc.sync.dma_start(plane[r:P:32, :, :].bitcast(I32), rows[r].bitcast(I32))
+
+        def load_words(name, src, e0, e1):
+            t = keep.tile([P, e1 - e0, 2 * H], U8, name=name, align_bytes=64)
+            nc.sync.dma_start(t[:].bitcast(I32), src[e0:e1, 0].rearrange("e p b -> p e b").bitcast(I32))
+            return [t[:, e - e0, :] for e in range(e0, e1)]
+
+        x_plane = keep.tile([P, T], U8, name="x_plane", align_bytes=64)
+        nc.gpsimd.memset(x_plane[:].bitcast(I32), 0)
+        w1_plane = zeroed_plane("w1_plane", [P, E, H])
+        wp_plane = zeroed_plane("wp_plane", [P, E, H])
+        w2_plane = zeroed_plane("w2_plane", [P, E, N])
+
+        token_list = load_list("token_list", offs)
+        x_table = keep.tile([P, T], U32, name="x_table")
+        nc.sync.dma_start(x_table[:].bitcast(I32), x_words[0].rearrange("p t d -> p (t d)").bitcast(I32))
+        partner_list = load_list("partner_list", offs2)
+        x_rows = x_scales[0].rearrange("(Q r) t -> r Q t", r=4)
+        for r in range(4):
+            nc.sync.dma_start(x_plane[r:P:32, :].bitcast(I32), x_rows[r].bitcast(I32))
+        w1 = []
+        wp = []
+
+        def load_first_layer(g):
+            e0, e1 = spans(LOAD_GROUPS)[g]
+            w1.extend(load_words("w1_slot%d" % (g % LOAD_SLOTS), w1_words, e0, e1))
+            wp.extend(load_words("wp_slot%d" % (g % LOAD_SLOTS), wp_words, e0, e1))
+
+        load_first_layer(0)
+        load_plane(w1_plane, w1_scales)
+        load_plane(wp_plane, wp_scales)
+        for g in range(1, LOAD_SLOTS):
+            load_first_layer(g)
+        load_plane(w2_plane, w2_scales)
+        slot_lists = [load_list("slot_list%d" % r, p) for r, p in enumerate((pos1, pos2, pos3))]
+
+        ident = keep.tile([P, P], F32, name="ident")
+        make_identity(nc, ident[:])
+
+        gathered = []
+
+        def gather(g):
+            e0, e1 = spans(GATHER_GROUPS)[g]
+            width = (e1 - e0) * C
+            cols = slice(e0 * C // 16, e1 * C // 16)
+            group = []
+            for name, table, dtype in (("words", x_table, U32), ("scales", x_plane, U8)):
+                for side, lst in (("tok", token_list), ("par", partner_list)):
+                    t = keep.tile([P, width], dtype, name="%s_%s_%d" % (side, name, g % GATHER_SLOTS), align_bytes=64)
+                    nc.vector.tensor_copy(t[:], table[:].indirect(lst[:, cols]))
+                    group.append(t)
+            for e in range(e0, e1):
+                gathered.append([t[:, (e - e0) * C : (e - e0 + 1) * C] for t in group])
+
+        for g in range(GATHER_SLOTS):
+            gather(g)
+
+        h_tiles = []
+        h_view = []
+        for e0, e1 in spans(QUANT_GROUPS):
+            t = keep.tile([P, (e1 - e0) * C, 4], BF16, name="h_%d" % e0, align_bytes=64)
+            h_tiles.append(t)
+            h_view.extend(t[:, (e - e0) * C : (e - e0 + 1) * C, :] for e in range(e0, e1))
+
+        relu = []
+
+        def first_layer(e):
+            tok_words, par_words, tok_scales, par_scales = gathered[e]
+            pre = bank(e % 3, [P, H])
+            nc.tensor.matmul_mx(out=pre[:], lhsT=tok_words.bitcast(FP8X4), lhsT_scale=tok_scales,
+                                rhs=w1[e].bitcast(FP4X4), rhs_scale=w1_plane[:, e, :], start=True, stop=False)
+            nc.tensor.matmul_mx(out=pre[:], lhsT=par_words.bitcast(FP8X4), lhsT_scale=par_scales,
+                                rhs=wp[e].bitcast(FP4X4), rhs_scale=wp_plane[:, e, :], start=False, stop=True)
+            r = ring.tile([P, 4, P], F32, name="relu")
+            nc.scalar.activation(r[:], pre[:].rearrange("s (q t) -> s t q", t=4), ACT.Relu)
+            relu.append(r)
+
+        def turn_and_square(e):
+            turned = bank(3 + e % 2, [P, 4, C])
+            for t in range(4):
+                nc.tensor.transpose(turned[:, t, :], relu[e][:, t, :], ident[:])
+            nc.scalar.activation(h_view[e], turned[:].rearrange("q t s -> q s t"), ACT.Square)
+
+        load_ends = [e1 for e0, e1 in spans(LOAD_GROUPS)]
+        gather_ends = [e1 for e0, e1 in spans(GATHER_GROUPS)]
+        w2 = []
+        for e in range(E):
+            first_layer(e)
+            if e + 1 in gather_ends[: len(GATHER_GROUPS) - GATHER_SLOTS]:
+                gather(gather_ends.index(e + 1) + GATHER_SLOTS)
+            if e + 1 in load_ends[: len(LOAD_GROUPS) - LOAD_SLOTS]:
+                load_first_layer(load_ends.index(e + 1) + LOAD_SLOTS)
+            if e == 5:
+                w2.extend(load_words("w1_slot0", w2_words, 0, E // 2))
+                w2.extend(load_words("wp_slot0", w2_words, E // 2, E))
+            if e == 8:
+                gates = keep.tile([P, TOP, T], F32, name="w1_slot1", align_bytes=64)
+                nc.sync.dma_start(gates[:], gate.rearrange("r p t -> p r t"))
+            if e > 0:
+                turn_and_square(e - 1)
+        turn_and_square(E - 1)
+
+        h_codes = []
+        h_scales = []
+
+        def quantise(g):
+            e0, e1 = spans(QUANT_GROUPS)[g]
+            codes = keep.tile([P, (e1 - e0) * C], U32, name="h_codes_%d" % e0, align_bytes=64)
+            scales = keep.tile([P, (e1 - e0) * C], U8, name="h_scales_%d" % e0, align_bytes=64)
+            nc.vector.quantize_mx(out=codes[:].bitcast(FP8X4), scales=scales[:],
+                                  in_=h_tiles[g][:].rearrange("p s t -> p (s t)"))
+            h_codes.extend(codes[:, (e - e0) * C : (e - e0 + 1) * C] for e in range(e0, e1))
+            h_scales.extend(scales[:, (e - e0) * C : (e - e0 + 1) * C] for e in range(e0, e1))
+
+        y = [keep.tile([P, S], F32, name="y_%d" % nb) for nb in range(NB)]
+
+        def second_layer(nb, e0, e1, b, on_vector):
+            acc = bank(b, [P, (e1 - e0) * C])
+            for e in range(e0, e1):
+                nc.tensor.matmul_mx(out=acc[:, (e - e0) * C : (e - e0 + 1) * C],
+                                    lhsT=w2[e][:, 2 * nb * P : 2 * (nb + 1) * P].bitcast(FP4X4),
+                                    lhsT_scale=w2_plane[:, e, nb * P : (nb + 1) * P],
+                                    rhs=h_codes[e].bitcast(FP8X4), rhs_scale=h_scales[e], start=True, stop=True)
+            if on_vector:
+                nc.vector.tensor_copy(y[nb][:, e0 * C : e1 * C], acc[:])
+            else:
+                nc.scalar.copy(y[nb][:, e0 * C : e1 * C], acc[:])
+
+        quantise(0)
+        second_layer(0, 0, 4, 0, True)
+        quantise(1)
+        second_layer(0, 4, 8, 1, True)
+        quantise(2)
+        second_layer(0, 8, 11, 5, True)
+        quantise(3)
+        second_layer(0, 11, 12, 6, True)
+        for nb in range(1, NB):
+            for g in range(3):
+                second_layer(nb, 4 * g, 4 * g + 4, (4, 3, 2)[g], False)
+
+        for nb in range(NB):
+            parts = []
+            for r in range(TOP):
+                part = ring.tile([P, T], F32, name="part%d" % r)
+                nc.vector.tensor_tensor(part[:], y[nb][:].indirect(slot_lists[r][:]), gates[:, r, :], ALU.mult)
+                parts.append(part)
+                if nb == NB - 1 and r == 1:
+                    pair = keep.tile([P, T], F32, name="pair")
+                    nc.vector.tensor_tensor(pair[:], parts[0][:], parts[1][:], ALU.add)
+            result = ring.tile([P, T], F32, name="result")
+            if nb == NB - 1:
+                nc.vector.tensor_tensor(result[:], pair[:], parts[2][:], ALU.add)
+            else:
+                summed = bank(5 + nb % 2, [P, T // P, P])
+                for tb in range(T // P):
+                    for r in range(TOP):
+                        nc.tensor.matmul(summed[:, tb, :], parts[r][:, tb * P : (tb + 1) * P], ident[:],
+                                         start=(r == 0), stop=(r == TOP - 1), is_transpose=True)
+                staged = ring.tile([P, T // P, P], F32, name="staged")
+                nc.scalar.copy(staged[:], summed[:])
+                back = bank((7, 0)[nb % 2], [P, T // P, P])
+                for tb in range(T // P):
+                    nc.tensor.transpose(back[:, tb, :], staged[:, tb, :], ident[:])
+                nc.scalar.copy(result[:], back[:].rearrange("n b t -> n (b t)"))
+            nc.sync.dma_start(out[nb * P : (nb + 1) * P, :], result[:])

@@ -22,7 +22,8 @@ P = 128
 NB = N // P
 GATHER_GROUPS = (1, 2, 2, 2, 2, 2, 1)
 GATHER_SLOTS = 2
-LOAD_GROUPS = (1, 1, 2, 2, 3, 3)
+LOAD_GROUPS = (2, 2, 2, 3, 3)
+PLANE_GROUPS = (4, 8)
 LOAD_SLOTS = 3
 QUANT_GROUPS = (8, 2, 1, 1)
 
@@ -54,10 +55,11 @@ def tile_moe_duo_relu2_kernel(
             nc.vector.memset(t[:].bitcast(I32), 0)
             return t
 
-        def load_plane(plane, src):
-            rows = src[:, 0].rearrange("e (Q r) n -> r Q e n", r=4)
+        def load_plane(plane, src, e0, e1):
+            rows = src[e0:e1, 0].rearrange("e (Q r) n -> r Q e n", r=4)
             for r in range(4):
                 nc.sync.dma_start(plane[r:P:32, :, :].bitcast(I32), rows[r].bitcast(I32))
+            return [plane[:, e - e0, :] for e in range(e0, e1)]
 
         def load_words(name, src, e0, e1):
             t = keep.tile([P, e1 - e0, 2 * H], U8, name=name, align_bytes=64)
@@ -66,9 +68,10 @@ def tile_moe_duo_relu2_kernel(
 
         x_plane = keep.tile([P, T], U8, name="x_plane", align_bytes=64)
         nc.gpsimd.memset(x_plane[:].bitcast(I32), 0)
-        w1_plane = zeroed_plane("w1_plane", [P, E, H])
-        wp_plane = zeroed_plane("wp_plane", [P, E, H])
-        w2_plane = zeroed_plane("w2_plane", [P, E, N])
+        first_planes = [
+            [zeroed_plane("%s_plane_%d" % (name, e0), [P, e1 - e0, H]) for name in ("w1", "wp")]
+            for e0, e1 in spans(PLANE_GROUPS)
+        ]
 
         token_list = load_list("token_list", offs)
         x_table = keep.tile([P, T], U32, name="x_table")
@@ -86,15 +89,24 @@ def tile_moe_duo_relu2_kernel(
             wp.extend(load_words("wp_slot%d" % (g % LOAD_SLOTS), wp_words, e0, e1))
 
         load_first_layer(0)
-        load_plane(w1_plane, w1_scales)
-        load_plane(wp_plane, wp_scales)
+        w1_plane = []
+        wp_plane = []
+
+        def load_first_planes(g):
+            e0, e1 = spans(PLANE_GROUPS)[g]
+            w1_plane.extend(load_plane(first_planes[g][0], w1_scales, e0, e1))
+            wp_plane.extend(load_plane(first_planes[g][1], wp_scales, e0, e1))
+
+        load_first_planes(0)
         for g in range(1, LOAD_SLOTS):
             load_first_layer(g)
-        load_plane(w2_plane, w2_scales)
-        slot_lists = [load_list("slot_list%d" % r, p) for r, p in enumerate((pos1, pos2, pos3))]
-
+        load_first_planes(1)
         ident = keep.tile([P, P], F32, name="ident")
         make_identity(nc, ident[:])
+        w2_plane = keep.tile([P, E, N], U8, name="w2_plane", align_bytes=64)
+        nc.gpsimd.memset(w2_plane[:].bitcast(I32), 0)
+        load_plane(w2_plane, w2_scales, 0, E)
+        slot_lists = [load_list("slot_list%d" % r, p) for r, p in enumerate((pos1, pos2, pos3))]
 
         gathered = []
 
@@ -103,8 +115,8 @@ def tile_moe_duo_relu2_kernel(
             width = (e1 - e0) * C
             cols = slice(e0 * C // 16, e1 * C // 16)
             group = []
-            for name, table, dtype in (("words", x_table, U32), ("scales", x_plane, U8)):
-                for side, lst in (("tok", token_list), ("par", partner_list)):
+            for side, lst in (("tok", token_list), ("par", partner_list)):
+                for name, table, dtype in (("words", x_table, U32), ("scales", x_plane, U8)):
                     t = keep.tile([P, width], dtype, name="%s_%s_%d" % (side, name, g % GATHER_SLOTS), align_bytes=64)
                     nc.vector.tensor_copy(t[:], table[:].indirect(lst[:, cols]))
                     group.append(t)
@@ -124,21 +136,26 @@ def tile_moe_duo_relu2_kernel(
         relu = []
 
         def first_layer(e):
-            tok_words, par_words, tok_scales, par_scales = gathered[e]
+            tok_words, tok_scales, par_words, par_scales = gathered[e]
             pre = bank(e % 3, [P, H])
             nc.tensor.matmul_mx(out=pre[:], lhsT=tok_words.bitcast(FP8X4), lhsT_scale=tok_scales,
-                                rhs=w1[e].bitcast(FP4X4), rhs_scale=w1_plane[:, e, :], start=True, stop=False)
+                                rhs=w1[e].bitcast(FP4X4), rhs_scale=w1_plane[e], start=True, stop=False)
             nc.tensor.matmul_mx(out=pre[:], lhsT=par_words.bitcast(FP8X4), lhsT_scale=par_scales,
-                                rhs=wp[e].bitcast(FP4X4), rhs_scale=wp_plane[:, e, :], start=False, stop=True)
-            r = ring.tile([P, 4, P], F32, name="relu")
+                                rhs=wp[e].bitcast(FP4X4), rhs_scale=wp_plane[e], start=False, stop=True)
+            r = ring.tile([P, 4, P], F32, name="relu", bufs=4)
             nc.scalar.activation(r[:], pre[:].rearrange("s (q t) -> s t q", t=4), ACT.Relu)
             relu.append(r)
 
-        def turn_and_square(e):
-            turned = bank(3 + e % 2, [P, 4, C])
+        turned = []
+
+        def turn(e):
+            tile = bank((3, 4, 7)[e % 3], [P, 4, C])
             for t in range(4):
-                nc.tensor.transpose(turned[:, t, :], relu[e][:, t, :], ident[:])
-            nc.scalar.activation(h_view[e], turned[:].rearrange("q t s -> q s t"), ACT.Square)
+                nc.tensor.transpose(tile[:, t, :], relu[e][:, t, :], ident[:])
+            turned.append(tile)
+
+        def square(e):
+            nc.scalar.activation(h_view[e], turned[e][:].rearrange("q t s -> q s t"), ACT.Square)
 
         load_ends = [e1 for e0, e1 in spans(LOAD_GROUPS)]
         gather_ends = [e1 for e0, e1 in spans(GATHER_GROUPS)]
@@ -150,14 +167,18 @@ def tile_moe_duo_relu2_kernel(
             if e + 1 in load_ends[: len(LOAD_GROUPS) - LOAD_SLOTS]:
                 load_first_layer(load_ends.index(e + 1) + LOAD_SLOTS)
             if e == 5:
-                w2.extend(load_words("w1_slot0", w2_words, 0, E // 2))
-                w2.extend(load_words("wp_slot0", w2_words, E // 2, E))
+                w2.extend(load_words("w1_slot2", w2_words, 0, E // 2))
+                w2.extend(load_words("wp_slot2", w2_words, E // 2, E))
             if e == 8:
-                gates = keep.tile([P, TOP, T], F32, name="w1_slot1", align_bytes=64)
+                gates = keep.tile([P, TOP, T], F32, name="w1_slot0", align_bytes=64)
                 nc.sync.dma_start(gates[:], gate.rearrange("r p t -> p r t"))
             if e > 0:
-                turn_and_square(e - 1)
-        turn_and_square(E - 1)
+                turn(e - 1)
+            if e > 1:
+                square(e - 2)
+        turn(E - 1)
+        square(E - 2)
+        square(E - 1)
 
         h_codes = []
         h_scales = []
@@ -190,35 +211,45 @@ def tile_moe_duo_relu2_kernel(
         quantise(1)
         second_layer(0, 4, 8, 1, True)
         quantise(2)
-        second_layer(0, 8, 11, 5, True)
+        second_layer(0, 8, 11, 5, False)
         quantise(3)
         second_layer(0, 11, 12, 6, True)
         for nb in range(1, NB):
             for g in range(3):
-                second_layer(nb, 4 * g, 4 * g + 4, (4, 3, 2)[g], False)
+                second_layer(nb, 4 * g, 4 * g + 4, (7, 5, 6)[g], False)
 
-        for nb in range(NB):
-            parts = []
+        def weighted_pick(nb, r, part, t0, t1):
+            nc.vector.tensor_tensor(part[:, t0:t1], y[nb][:].indirect(slot_lists[r][:, t0 // 16 : t1 // 16]),
+                                    gates[:, r, t0:t1], ALU.mult)
+
+        for nb in range(NB - 1):
+            parts = [ring.tile([P, T], F32, name="part%d" % r) for r in range(TOP)]
             for r in range(TOP):
-                part = ring.tile([P, T], F32, name="part%d" % r)
-                nc.vector.tensor_tensor(part[:], y[nb][:].indirect(slot_lists[r][:]), gates[:, r, :], ALU.mult)
-                parts.append(part)
-                if nb == NB - 1 and r == 1:
-                    pair = keep.tile([P, T], F32, name="pair")
-                    nc.vector.tensor_tensor(pair[:], parts[0][:], parts[1][:], ALU.add)
+                weighted_pick(nb, r, parts[r], 0, T)
+            summed = bank(nb % 2, [P, T // P, P])
+            for tb in range(T // P):
+                for r in range(TOP):
+                    nc.tensor.matmul(summed[:, tb, :], parts[r][:, tb * P : (tb + 1) * P], ident[:],
+                                     start=(r == 0), stop=(r == TOP - 1), is_transpose=True)
+            staged = ring.tile([P, T // P, P], F32, name="staged")
+            nc.scalar.copy(staged[:], summed[:])
+            back = bank(2 + nb % 2, [P, T // P, P])
+            for tb in range(T // P):
+                nc.tensor.transpose(back[:, tb, :], staged[:, tb, :], ident[:])
             result = ring.tile([P, T], F32, name="result")
-            if nb == NB - 1:
-                nc.vector.tensor_tensor(result[:], pair[:], parts[2][:], ALU.add)
-            else:
-                summed = bank(5 + nb % 2, [P, T // P, P])
-                for tb in range(T // P):
-                    for r in range(TOP):
-                        nc.tensor.matmul(summed[:, tb, :], parts[r][:, tb * P : (tb + 1) * P], ident[:],
-                                         start=(r == 0), stop=(r == TOP - 1), is_transpose=True)
-                staged = ring.tile([P, T // P, P], F32, name="staged")
-                nc.scalar.copy(staged[:], summed[:])
-                back = bank((7, 0)[nb % 2], [P, T // P, P])
-                for tb in range(T // P):
-                    nc.tensor.transpose(back[:, tb, :], staged[:, tb, :], ident[:])
-                nc.scalar.copy(result[:], back[:].rearrange("n b t -> n (b t)"))
+            nc.scalar.copy(result[:], back[:].rearrange("n b t -> n (b t)"))
             nc.sync.dma_start(out[nb * P : (nb + 1) * P, :], result[:])
+
+        nb = NB - 1
+        half = T // 2
+        parts = [ring.tile([P, T], F32, name="part%d" % r) for r in range(TOP)]
+        pair = keep.tile([P, T], F32, name="pair")
+        weighted_pick(nb, 0, parts[0], 0, T)
+        weighted_pick(nb, 1, parts[1], 0, T)
+        weighted_pick(nb, 2, parts[2], 0, half)
+        nc.vector.tensor_tensor(pair[:], parts[0][:], parts[1][:], ALU.add)
+        weighted_pick(nb, 2, parts[2], half, T)
+        for t0 in (0, half):
+            result = ring.tile([P, half], F32, name="result")
+            nc.vector.tensor_tensor(result[:], pair[:, t0 : t0 + half], parts[2][:, t0 : t0 + half], ALU.add)
+            nc.sync.dma_start(out[nb * P : (nb + 1) * P, t0 : t0 + half], result[:])

@@ -20,10 +20,11 @@ ALU = mybir.AluOpType
 
 P = 128
 NB = N // P
-GATHER_GROUPS = (1, 2, 2, 2, 2, 2, 1)
+WORD_GROUPS = (1, 2, 2, 2, 2, 2, 1)
+SCALE_GROUPS = (1, 2, 3, 3, 3)
 GATHER_SLOTS = 2
 LOAD_GROUPS = (2, 2, 2, 3, 3)
-PLANE_GROUPS = (4, 8)
+PLANE_GROUPS = (6, 6)
 LOAD_SLOTS = 3
 QUANT_GROUPS = (8, 2, 1, 1)
 
@@ -50,9 +51,9 @@ def tile_moe_duo_relu2_kernel(
             nc.sync.dma_start(t[:], src)
             return t
 
-        def zeroed_plane(name, shape):
+        def zeroed_plane(name, shape, engine):
             t = keep.tile(shape, U8, name=name, align_bytes=64)
-            nc.vector.memset(t[:].bitcast(I32), 0)
+            engine.memset(t[:].bitcast(I32), 0)
             return t
 
         def load_plane(plane, src, e0, e1):
@@ -66,10 +67,10 @@ def tile_moe_duo_relu2_kernel(
             nc.sync.dma_start(t[:].bitcast(I32), src[e0:e1, 0].rearrange("e p b -> p e b").bitcast(I32))
             return [t[:, e - e0, :] for e in range(e0, e1)]
 
-        x_plane = keep.tile([P, T], U8, name="x_plane", align_bytes=64)
-        nc.gpsimd.memset(x_plane[:].bitcast(I32), 0)
+        x_plane = zeroed_plane("x_plane", [P, T], nc.gpsimd)
         first_planes = [
-            [zeroed_plane("%s_plane_%d" % (name, e0), [P, e1 - e0, H]) for name in ("w1", "wp")]
+            [zeroed_plane("%s_plane_%d" % (name, e0), [P, e1 - e0, H], engine)
+             for name, engine in (("w1", nc.vector), ("wp", nc.gpsimd))]
             for e0, e1 in spans(PLANE_GROUPS)
         ]
 
@@ -103,28 +104,28 @@ def tile_moe_duo_relu2_kernel(
         load_first_planes(1)
         ident = keep.tile([P, P], F32, name="ident")
         make_identity(nc, ident[:])
-        w2_plane = keep.tile([P, E, N], U8, name="w2_plane", align_bytes=64)
-        nc.gpsimd.memset(w2_plane[:].bitcast(I32), 0)
+        w2_plane = zeroed_plane("w2_plane", [P, E, N], nc.vector)
         load_plane(w2_plane, w2_scales, 0, E)
         slot_lists = [load_list("slot_list%d" % r, p) for r, p in enumerate((pos1, pos2, pos3))]
 
-        gathered = []
+        gathered = {"words": [], "scales": []}
+        sorts = {"words": (WORD_GROUPS, x_table, U32), "scales": (SCALE_GROUPS, x_plane, U8)}
 
-        def gather(g):
-            e0, e1 = spans(GATHER_GROUPS)[g]
-            width = (e1 - e0) * C
+        def gather(sort, g):
+            groups, table, dtype = sorts[sort]
+            e0, e1 = spans(groups)[g]
             cols = slice(e0 * C // 16, e1 * C // 16)
-            group = []
+            pair = []
             for side, lst in (("tok", token_list), ("par", partner_list)):
-                for name, table, dtype in (("words", x_table, U32), ("scales", x_plane, U8)):
-                    t = keep.tile([P, width], dtype, name="%s_%s_%d" % (side, name, g % GATHER_SLOTS), align_bytes=64)
-                    nc.vector.tensor_copy(t[:], table[:].indirect(lst[:, cols]))
-                    group.append(t)
+                t = keep.tile([P, (e1 - e0) * C], dtype, name="%s_%s_%d" % (side, sort, g % GATHER_SLOTS), align_bytes=64)
+                nc.vector.tensor_copy(t[:], table[:].indirect(lst[:, cols]))
+                pair.append(t)
             for e in range(e0, e1):
-                gathered.append([t[:, (e - e0) * C : (e - e0 + 1) * C] for t in group])
+                gathered[sort].append([t[:, (e - e0) * C : (e - e0 + 1) * C] for t in pair])
 
         for g in range(GATHER_SLOTS):
-            gather(g)
+            gather("words", g)
+            gather("scales", g)
 
         h_tiles = []
         h_view = []
@@ -136,7 +137,8 @@ def tile_moe_duo_relu2_kernel(
         relu = []
 
         def first_layer(e):
-            tok_words, tok_scales, par_words, par_scales = gathered[e]
+            tok_words, par_words = gathered["words"][e]
+            tok_scales, par_scales = gathered["scales"][e]
             pre = bank(e % 3, [P, H])
             nc.tensor.matmul_mx(out=pre[:], lhsT=tok_words.bitcast(FP8X4), lhsT_scale=tok_scales,
                                 rhs=w1[e].bitcast(FP4X4), rhs_scale=w1_plane[e], start=True, stop=False)
@@ -158,12 +160,13 @@ def tile_moe_duo_relu2_kernel(
             nc.scalar.activation(h_view[e], turned[e][:].rearrange("q t s -> q s t"), ACT.Square)
 
         load_ends = [e1 for e0, e1 in spans(LOAD_GROUPS)]
-        gather_ends = [e1 for e0, e1 in spans(GATHER_GROUPS)]
         w2 = []
         for e in range(E):
             first_layer(e)
-            if e + 1 in gather_ends[: len(GATHER_GROUPS) - GATHER_SLOTS]:
-                gather(gather_ends.index(e + 1) + GATHER_SLOTS)
+            for sort in ("words", "scales"):
+                ends = [e1 for e0, e1 in spans(sorts[sort][0])]
+                if e + 1 in ends[: len(ends) - GATHER_SLOTS]:
+                    gather(sort, ends.index(e + 1) + GATHER_SLOTS)
             if e + 1 in load_ends[: len(LOAD_GROUPS) - LOAD_SLOTS]:
                 load_first_layer(load_ends.index(e + 1) + LOAD_SLOTS)
             if e == 5:
@@ -222,26 +225,28 @@ def tile_moe_duo_relu2_kernel(
             nc.vector.tensor_tensor(part[:, t0:t1], y[nb][:].indirect(slot_lists[r][:, t0 // 16 : t1 // 16]),
                                     gates[:, r, t0:t1], ALU.mult)
 
+        half = T // 2
         for nb in range(NB - 1):
             parts = [ring.tile([P, T], F32, name="part%d" % r) for r in range(TOP)]
             for r in range(TOP):
                 weighted_pick(nb, r, parts[r], 0, T)
-            summed = bank(nb % 2, [P, T // P, P])
-            for tb in range(T // P):
-                for r in range(TOP):
-                    nc.tensor.matmul(summed[:, tb, :], parts[r][:, tb * P : (tb + 1) * P], ident[:],
-                                     start=(r == 0), stop=(r == TOP - 1), is_transpose=True)
-            staged = ring.tile([P, T // P, P], F32, name="staged")
-            nc.scalar.copy(staged[:], summed[:])
-            back = bank(2 + nb % 2, [P, T // P, P])
-            for tb in range(T // P):
-                nc.tensor.transpose(back[:, tb, :], staged[:, tb, :], ident[:])
-            result = ring.tile([P, T], F32, name="result")
-            nc.scalar.copy(result[:], back[:].rearrange("n b t -> n (b t)"))
-            nc.sync.dma_start(out[nb * P : (nb + 1) * P, :], result[:])
+            for u in range(2):
+                summed = bank(u, [P, 2, P])
+                for j in range(2):
+                    tb = 2 * u + j
+                    for r in range(TOP):
+                        nc.tensor.matmul(summed[:, j, :], parts[r][:, tb * P : (tb + 1) * P], ident[:],
+                                         start=(r == 0), stop=(r == TOP - 1), is_transpose=True)
+                staged = ring.tile([P, 2, P], F32, name="staged")
+                nc.scalar.copy(staged[:], summed[:])
+                back = bank(2 + u, [P, 2, P])
+                for j in range(2):
+                    nc.tensor.transpose(back[:, j, :], staged[:, j, :], ident[:])
+                result = ring.tile([P, half], F32, name="result")
+                nc.scalar.copy(result[:], back[:].rearrange("n b t -> n (b t)"))
+                nc.sync.dma_start(out[nb * P : (nb + 1) * P, u * half : (u + 1) * half], result[:])
 
         nb = NB - 1
-        half = T // 2
         parts = [ring.tile([P, T], F32, name="part%d" % r) for r in range(TOP)]
         pair = keep.tile([P, T], F32, name="pair")
         weighted_pick(nb, 0, parts[0], 0, T)

@@ -20,13 +20,14 @@ ALU = mybir.AluOpType
 
 P = 128
 NB = N // P
-WORD_GROUPS = (1, 2, 2, 2, 2, 2, 1)
-SCALE_GROUPS = (1, 2, 3, 3, 3)
-GATHER_SLOTS = 2
-LOAD_GROUPS = (2, 2, 2, 3, 3)
+WORD_GROUPS = (1, 1, 1, 2, 2, 2, 1, 1, 1)
+SCALE_GROUPS = (1, 2, 2, 2, 2, 1, 1, 1)
+GATHER_SLOTS = {"words": 3, "scales": 3}
+LOAD_GROUPS = (2, 2, 2, 2, 2, 2)
 PLANE_GROUPS = (6, 6)
-LOAD_SLOTS = 3
-QUANT_GROUPS = (8, 2, 1, 1)
+QUANT_GROUPS = (4, 4, 3, 1)
+PRE_BANKS = (0, 1, 2, 0, 1, 2, 0, 1, 2, 0, 1, 2)
+TURN_BANKS = (3, 4, 5, 3, 4, 5, 3, 4, 5, 3, 4, 5)
 
 
 def spans(sizes):
@@ -59,20 +60,38 @@ def tile_moe_duo_relu2_kernel(
         def load_plane(plane, src, e0, e1):
             rows = src[e0:e1, 0].rearrange("e (Q r) n -> r Q e n", r=4)
             for r in range(4):
-                nc.sync.dma_start(plane[r:P:32, :, :].bitcast(I32), rows[r].bitcast(I32))
-            return [plane[:, e - e0, :] for e in range(e0, e1)]
+                nc.sync.dma_start(plane[r:P:32, :].rearrange("p (e n) -> p e n", n=H).bitcast(I32), rows[r].bitcast(I32))
+            return [plane[:, (e - e0) * H : (e - e0 + 1) * H] for e in range(e0, e1)]
 
-        def load_words(name, src, e0, e1):
-            t = keep.tile([P, e1 - e0, 2 * H], U8, name=name, align_bytes=64)
-            nc.sync.dma_start(t[:].bitcast(I32), src[e0:e1, 0].rearrange("e p b -> p e b").bitcast(I32))
-            return [t[:, e - e0, :] for e in range(e0, e1)]
+        def load_words(t, src, e0, e1):
+            nc.sync.dma_start(t.rearrange("p (e b) -> p e b", b=2 * H).bitcast(I32),
+                              src[e0:e1, 0].rearrange("e p b -> p e b").bitcast(I32))
+            return [t[:, (e - e0) * 2 * H : (e - e0 + 1) * 2 * H] for e in range(e0, e1)]
 
+        (a0, a1), (b0, b1) = spans(PLANE_GROUPS)
         x_plane = zeroed_plane("x_plane", [P, T], nc.gpsimd)
-        first_planes = [
-            [zeroed_plane("%s_plane_%d" % (name, e0), [P, e1 - e0, H], engine)
-             for name, engine in (("w1", nc.vector), ("wp", nc.gpsimd))]
-            for e0, e1 in spans(PLANE_GROUPS)
-        ]
+        ident = keep.tile([P, P], F32, name="ident")
+        make_identity(nc, ident[:])
+        gate_rows = keep.tile([P, P], F32, name="gate_rows")
+        nc.gpsimd.memset(gate_rows[:], 0.0)
+        w1_plane_a = zeroed_plane("w1_plane_a", [P, (a1 - a0) * H], nc.vector)
+        wp_plane_a = zeroed_plane("wp_plane_a", [P, (a1 - a0) * H], nc.vector)
+        wp_plane_b = zeroed_plane("wp_plane_b", [P, (b1 - b0) * H], nc.vector)
+        w1_plane_b = zeroed_plane("w1_plane_b", [P, (b1 - b0) * H], nc.gpsimd)
+
+
+        early = keep.tile([P, E * N], U8, name="early", align_bytes=64)
+        places = {("w1", 0): early[:, 0:2048], ("wp", 0): early[:, 2048:4096], ("wp", 1): early[:, 4096:6144]}
+        w1 = []
+        wp = []
+
+        def load_group(name, g):
+            e0, e1 = spans(LOAD_GROUPS)[g]
+            if (name, g) not in places:
+                t = keep.tile([P, (e1 - e0) * 2 * H], U8, name="%s_%d" % (name, g), align_bytes=64)
+                places[name, g] = t[:]
+            dst, src = {"w1": (w1, w1_words), "wp": (wp, wp_words)}[name]
+            dst.extend(load_words(places[name, g], src, e0, e1))
 
         token_list = load_list("token_list", offs)
         x_table = keep.tile([P, T], U32, name="x_table")
@@ -80,33 +99,22 @@ def tile_moe_duo_relu2_kernel(
         partner_list = load_list("partner_list", offs2)
         x_rows = x_scales[0].rearrange("(Q r) t -> r Q t", r=4)
         for r in range(4):
+            if r == 3:
+                load_group("w1", 0)
+                load_group("wp", 0)
             nc.sync.dma_start(x_plane[r:P:32, :].bitcast(I32), x_rows[r].bitcast(I32))
-        w1 = []
-        wp = []
-
-        def load_first_layer(g):
-            e0, e1 = spans(LOAD_GROUPS)[g]
-            w1.extend(load_words("w1_slot%d" % (g % LOAD_SLOTS), w1_words, e0, e1))
-            wp.extend(load_words("wp_slot%d" % (g % LOAD_SLOTS), wp_words, e0, e1))
-
-        load_first_layer(0)
-        w1_plane = []
-        wp_plane = []
-
-        def load_first_planes(g):
-            e0, e1 = spans(PLANE_GROUPS)[g]
-            w1_plane.extend(load_plane(first_planes[g][0], w1_scales, e0, e1))
-            wp_plane.extend(load_plane(first_planes[g][1], wp_scales, e0, e1))
-
-        load_first_planes(0)
-        for g in range(1, LOAD_SLOTS):
-            load_first_layer(g)
-        load_first_planes(1)
-        ident = keep.tile([P, P], F32, name="ident")
-        make_identity(nc, ident[:])
-        w2_plane = zeroed_plane("w2_plane", [P, E, N], nc.vector)
-        load_plane(w2_plane, w2_scales, 0, E)
-        slot_lists = [load_list("slot_list%d" % r, p) for r, p in enumerate((pos1, pos2, pos3))]
+        w1_plane = load_plane(w1_plane_a, w1_scales, a0, a1)
+        wp_plane = load_plane(wp_plane_a, wp_scales, a0, a1)
+        for g in (1, 2):
+            load_group("wp", g)
+            load_group("w1", g)
+        wp_plane.extend(load_plane(wp_plane_b, wp_scales, b0, b1))
+        load_group("wp", 3)
+        w1_plane.extend(load_plane(w1_plane_b, w1_scales, b0, b1))
+        load_group("w1", 3)
+        for g in (4, 5):
+            load_group("wp", g)
+            load_group("w1", g)
 
         gathered = {"words": [], "scales": []}
         sorts = {"words": (WORD_GROUPS, x_table, U32), "scales": (SCALE_GROUPS, x_plane, U8)}
@@ -117,15 +125,15 @@ def tile_moe_duo_relu2_kernel(
             cols = slice(e0 * C // 16, e1 * C // 16)
             pair = []
             for side, lst in (("tok", token_list), ("par", partner_list)):
-                t = keep.tile([P, (e1 - e0) * C], dtype, name="%s_%s_%d" % (side, sort, g % GATHER_SLOTS), align_bytes=64)
+                t = keep.tile([P, (e1 - e0) * C], dtype, name="%s_%s_%d" % (side, sort, g % GATHER_SLOTS[sort]), align_bytes=64)
                 nc.vector.tensor_copy(t[:], table[:].indirect(lst[:, cols]))
                 pair.append(t)
             for e in range(e0, e1):
                 gathered[sort].append([t[:, (e - e0) * C : (e - e0 + 1) * C] for t in pair])
 
-        for g in range(GATHER_SLOTS):
-            gather("words", g)
-            gather("scales", g)
+        for sort in ("words", "scales"):
+            for g in range(GATHER_SLOTS[sort]):
+                gather(sort, g)
 
         h_tiles = []
         h_view = []
@@ -139,19 +147,23 @@ def tile_moe_duo_relu2_kernel(
         def first_layer(e):
             tok_words, par_words = gathered["words"][e]
             tok_scales, par_scales = gathered["scales"][e]
-            pre = bank(e % 3, [P, H])
+            pre = bank(PRE_BANKS[e], [P, H])
             nc.tensor.matmul_mx(out=pre[:], lhsT=tok_words.bitcast(FP8X4), lhsT_scale=tok_scales,
                                 rhs=w1[e].bitcast(FP4X4), rhs_scale=w1_plane[e], start=True, stop=False)
             nc.tensor.matmul_mx(out=pre[:], lhsT=par_words.bitcast(FP8X4), lhsT_scale=par_scales,
                                 rhs=wp[e].bitcast(FP4X4), rhs_scale=wp_plane[e], start=False, stop=True)
             r = ring.tile([P, 4, P], F32, name="relu", bufs=4)
-            nc.scalar.activation(r[:], pre[:].rearrange("s (q t) -> s t q", t=4), ACT.Relu)
+            stepped = pre[:].rearrange("s (q t) -> s t q", t=4)
+            if e >= E - 3:
+                nc.vector.tensor_scalar(r[:], stepped, 0.0, None, ALU.max)
+            else:
+                nc.scalar.activation(r[:], stepped, ACT.Relu)
             relu.append(r)
 
         turned = []
 
         def turn(e):
-            tile = bank((3, 4, 7)[e % 3], [P, 4, C])
+            tile = bank(TURN_BANKS[e], [P, 4, C])
             for t in range(4):
                 nc.tensor.transpose(tile[:, t, :], relu[e][:, t, :], ident[:])
             turned.append(tile)
@@ -159,41 +171,42 @@ def tile_moe_duo_relu2_kernel(
         def square(e):
             nc.scalar.activation(h_view[e], turned[e][:].rearrange("q t s -> q s t"), ACT.Square)
 
-        load_ends = [e1 for e0, e1 in spans(LOAD_GROUPS)]
-        w2 = []
-        for e in range(E):
-            first_layer(e)
-            for sort in ("words", "scales"):
-                ends = [e1 for e0, e1 in spans(sorts[sort][0])]
-                if e + 1 in ends[: len(ends) - GATHER_SLOTS]:
-                    gather(sort, ends.index(e + 1) + GATHER_SLOTS)
-            if e + 1 in load_ends[: len(LOAD_GROUPS) - LOAD_SLOTS]:
-                load_first_layer(load_ends.index(e + 1) + LOAD_SLOTS)
-            if e == 5:
-                w2.extend(load_words("w1_slot2", w2_words, 0, E // 2))
-                w2.extend(load_words("wp_slot2", w2_words, E // 2, E))
-            if e == 8:
-                gates = keep.tile([P, TOP, T], F32, name="w1_slot0", align_bytes=64)
-                nc.sync.dma_start(gates[:], gate.rearrange("r p t -> p r t"))
-            if e > 0:
-                turn(e - 1)
-            if e > 1:
-                square(e - 2)
-        turn(E - 1)
-        square(E - 2)
-        square(E - 1)
-
         h_codes = []
         h_scales = []
 
         def quantise(g):
             e0, e1 = spans(QUANT_GROUPS)[g]
-            codes = keep.tile([P, (e1 - e0) * C], U32, name="h_codes_%d" % e0, align_bytes=64)
+            codes = keep.tile([P, (e1 - e0) * C], U32, name="h_codes_%d" % e0 if g != 1 else "par_words_2", align_bytes=64)
             scales = keep.tile([P, (e1 - e0) * C], U8, name="h_scales_%d" % e0, align_bytes=64)
             nc.vector.quantize_mx(out=codes[:].bitcast(FP8X4), scales=scales[:],
                                   in_=h_tiles[g][:].rearrange("p s t -> p (s t)"))
             h_codes.extend(codes[:, (e - e0) * C : (e - e0 + 1) * C] for e in range(e0, e1))
             h_scales.extend(scales[:, (e - e0) * C : (e - e0 + 1) * C] for e in range(e0, e1))
+
+        for e in range(E):
+            first_layer(e)
+            for sort in ("words", "scales"):
+                ends = [e1 for e0, e1 in spans(sorts[sort][0])]
+                if e + 1 in ends[: len(ends) - GATHER_SLOTS[sort]]:
+                    gather(sort, ends.index(e + 1) + GATHER_SLOTS[sort])
+            if e == 3:
+                w2_plane = load_plane(early, w2_scales, 0, E)
+                w2_tile = keep.tile([P, E * 2 * N], U8, name="w2", align_bytes=64)
+                w2 = load_words(w2_tile[:], w2_words, 0, E)
+                slot_lists = [load_list("slot_list%d" % r, p) for r, p in enumerate((pos1, pos2, pos3))]
+                gates = keep.tile([P, TOP, T], F32, name="gates")
+                nc.sync.dma_start(gates[:], gate.rearrange("r p t -> p r t"))
+                for r in range(2):
+                    nc.sync.dma_start(gate_rows[4 * r : 4 * r + 4, :], gate[r, 0, :].rearrange("(b t) -> b t", b=4))
+            for late in {2: (0,), 4: (1, 2), 6: (3, 4), 8: (5, 6), 9: (7,), 10: (8,), 11: (9,)}.get(e, ()):
+                turn(late)
+                square(late)
+            if e == 6:
+                quantise(0)
+        quantise(1)
+        for e in (E - 2, E - 1):
+            turn(e)
+            square(e)
 
         y = [keep.tile([P, S], F32, name="y_%d" % nb) for nb in range(NB)]
 
@@ -202,59 +215,88 @@ def tile_moe_duo_relu2_kernel(
             for e in range(e0, e1):
                 nc.tensor.matmul_mx(out=acc[:, (e - e0) * C : (e - e0 + 1) * C],
                                     lhsT=w2[e][:, 2 * nb * P : 2 * (nb + 1) * P].bitcast(FP4X4),
-                                    lhsT_scale=w2_plane[:, e, nb * P : (nb + 1) * P],
+                                    lhsT_scale=w2_plane[e][:, nb * P : (nb + 1) * P],
                                     rhs=h_codes[e].bitcast(FP8X4), rhs_scale=h_scales[e], start=True, stop=True)
             if on_vector:
                 nc.vector.tensor_copy(y[nb][:, e0 * C : e1 * C], acc[:])
             else:
                 nc.scalar.copy(y[nb][:, e0 * C : e1 * C], acc[:])
 
-        quantise(0)
-        second_layer(0, 0, 4, 0, True)
-        quantise(1)
-        second_layer(0, 4, 8, 1, True)
         quantise(2)
-        second_layer(0, 8, 11, 5, False)
+        second_layer(0, 0, 4, 0, True)
         quantise(3)
-        second_layer(0, 11, 12, 6, True)
-        for nb in range(1, NB):
+        second_layer(0, 4, 8, 4, False)
+        second_layer(0, 8, 11, 3, True)
+        second_layer(0, 11, 12, 6, False)
+        fills = {1: (4, 3, 0), 3: (6, 4, 3), 2: (0, 6, 4)}
+
+        def fill_block(nb):
             for g in range(3):
-                second_layer(nb, 4 * g, 4 * g + 4, (7, 5, 6)[g], False)
+                second_layer(nb, 4 * g, 4 * g + 4, fills[nb][g], False)
 
-        def weighted_pick(nb, r, part, t0, t1):
-            nc.vector.tensor_tensor(part[:, t0:t1], y[nb][:].indirect(slot_lists[r][:, t0 // 16 : t1 // 16]),
-                                    gates[:, r, t0:t1], ALU.mult)
+        def picked(nb, r):
+            return y[nb][:].indirect(slot_lists[r][:])
 
-        half = T // 2
-        for nb in range(NB - 1):
-            parts = [ring.tile([P, T], F32, name="part%d" % r) for r in range(TOP)]
-            for r in range(TOP):
-                weighted_pick(nb, r, parts[r], 0, T)
-            for u in range(2):
-                summed = bank(u, [P, 2, P])
-                for j in range(2):
-                    tb = 2 * u + j
-                    for r in range(TOP):
-                        nc.tensor.matmul(summed[:, j, :], parts[r][:, tb * P : (tb + 1) * P], ident[:],
-                                         start=(r == 0), stop=(r == TOP - 1), is_transpose=True)
-                staged = ring.tile([P, 2, P], F32, name="staged")
-                nc.scalar.copy(staged[:], summed[:])
-                back = bank(2 + u, [P, 2, P])
-                for j in range(2):
-                    nc.tensor.transpose(back[:, j, :], staged[:, j, :], ident[:])
-                result = ring.tile([P, half], F32, name="result")
-                nc.scalar.copy(result[:], back[:].rearrange("n b t -> n (b t)"))
-                nc.sync.dma_start(out[nb * P : (nb + 1) * P, u * half : (u + 1) * half], result[:])
+        def weighted_pick(nb, r):
+            part = keep.tile([P, T], F32, name="part%d" % (TOP * nb + r))
+            nc.vector.tensor_tensor(part[:], picked(nb, r), gates[:, r, :], ALU.mult)
+            return part
 
-        nb = NB - 1
-        parts = [ring.tile([P, T], F32, name="part%d" % r) for r in range(TOP)]
+        def turn_and_add(b, parts):
+            acc = bank(b, [P, NB, P])
+            for i, part in enumerate(parts):
+                for tb in range(NB):
+                    nc.tensor.matmul(acc[:, tb, :], part[:, tb * P : (tb + 1) * P], ident[:], is_transpose=True,
+                                     start=(i == 0 and tb == 0), stop=(i == len(parts) - 1 and tb == NB - 1))
+            return acc[:].rearrange("p b c -> p (b c)")
+
+        def copied(acc):
+            t = ring.tile([P, T], F32, name="staged", bufs=8)
+            nc.scalar.copy(t[:], acc)
+            return t
+
+        def store(nb, result, t0, t1):
+            nc.sync.dma_start(out[nb * P : (nb + 1) * P, t0:t1], result[:, t0:t1])
+
+        gate_bank = bank(7, [P, P])
+        nc.tensor.transpose(gate_bank[:], gate_rows[:], ident[:])
+        gate_cols = keep.tile([P, 8], F32, name="gate_cols")
+        nc.scalar.copy(gate_cols[:], gate_bank[:, 0:8])
+
+        def plain_pick(r):
+            part = keep.tile([P, T], F32, name="plain%d" % r)
+            nc.scalar.activation(part[:], picked(3, r), ACT.Copy)
+            return part
+
+        def weighted_copy(acc, r):
+            t = keep.tile([P, T], F32, name="weighted%d" % r)
+            for tb in range(NB):
+                nc.scalar.activation(t[:, tb * P : (tb + 1) * P], acc[:, tb * P : (tb + 1) * P], ACT.Copy,
+                                     scale=gate_cols[:, 4 * r + tb : 4 * r + tb + 1])
+            return t
+
+        fill_block(1)
+        parts = {(nb, r): weighted_pick(nb, r) for nb in range(2) for r in range(TOP)}
+        fill_block(3)
+        turned0 = turn_and_add(5, [plain_pick(0)])
+        fill_block(2)
+        parts.update({(2, r): weighted_pick(2, r) for r in range(TOP)})
+        plain1 = plain_pick(1)
+        sum0 = copied(turn_and_add(0, [parts[0, r] for r in range(TOP)]))
+        parts[3, 2] = weighted_pick(3, 2)
+        sum1 = copied(turn_and_add(6, [parts[1, r] for r in range(TOP)]))
+        turned1 = turn_and_add(7, [plain1])
+        store(0, copied(turn_and_add(1, [sum0])), 0, T)
+        weighted = [weighted_copy(turned0, 0)]
+        store(1, copied(turn_and_add(2, [sum1])), 0, T)
+        weighted.append(weighted_copy(turned1, 1))
         pair = keep.tile([P, T], F32, name="pair")
-        weighted_pick(nb, 0, parts[0], 0, T)
-        weighted_pick(nb, 1, parts[1], 0, T)
-        weighted_pick(nb, 2, parts[2], 0, half)
-        nc.vector.tensor_tensor(pair[:], parts[0][:], parts[1][:], ALU.add)
-        weighted_pick(nb, 2, parts[2], half, T)
-        for t0 in (0, half):
-            result = ring.tile([P, half], F32, name="result")
-            nc.vector.tensor_tensor(result[:], pair[:, t0 : t0 + half], parts[2][:, t0 : t0 + half], ALU.add)
-            nc.sync.dma_start(out[nb * P : (nb + 1) * P, t0 : t0 + half], result[:])
+        nc.vector.tensor_tensor(pair[:], parts[2, 0][:], parts[2, 1][:], ALU.add)
+        back = {3: turn_and_add(3, weighted), 2: pair}
+        half = T // 2
+        for nb in (3, 2):
+            result = keep.tile([P, T], F32, name={3: "result3", 2: "weighted1"}[nb])
+            for t0 in (0, half):
+                nc.vector.tensor_tensor(result[:, t0 : t0 + half], back[nb][:, t0 : t0 + half],
+                                        parts[nb, 2][:, t0 : t0 + half], ALU.add)
+                store(nb, result, t0, t0 + half)

@@ -20,11 +20,12 @@ ALU = mybir.AluOpType
 
 P = 128
 NB = N // P
-WORD_GROUPS = (1, 1, 1, 2, 2, 2, 1, 1, 1)
-SCALE_GROUPS = (1, 2, 2, 2, 2, 1, 1, 1)
-GATHER_SLOTS = {"words": 3, "scales": 3}
+WORD_GROUPS = (1, 2, 2, 2, 2, 2, 1)
+SCALE_GROUPS = (1, 2, 2, 2, 2, 2, 1)
+GATHER_SLOTS = {"words": 2, "scales": 2}
 LOAD_GROUPS = (2, 2, 2, 2, 2, 2)
 PLANE_GROUPS = (6, 6)
+SPLIT = 128
 QUANT_GROUPS = (4, 4, 3, 1)
 PRE_BANKS = (0, 1, 2, 0, 1, 2, 0, 1, 2, 0, 1, 2)
 TURN_BANKS = (3, 4, 5, 3, 4, 5, 3, 4, 5, 3, 4, 5)
@@ -154,7 +155,7 @@ def tile_moe_duo_relu2_kernel(
                                 rhs=wp[e].bitcast(FP4X4), rhs_scale=wp_plane[e], start=False, stop=True)
             r = ring.tile([P, 4, P], F32, name="relu", bufs=4)
             stepped = pre[:].rearrange("s (q t) -> s t q", t=4)
-            if e >= E - 3:
+            if e >= E - 2:
                 nc.vector.tensor_scalar(r[:], stepped, 0.0, None, ALU.max)
             else:
                 nc.scalar.activation(r[:], stepped, ACT.Relu)
@@ -176,7 +177,7 @@ def tile_moe_duo_relu2_kernel(
 
         def quantise(g):
             e0, e1 = spans(QUANT_GROUPS)[g]
-            codes = keep.tile([P, (e1 - e0) * C], U32, name="h_codes_%d" % e0 if g != 1 else "par_words_2", align_bytes=64)
+            codes = keep.tile([P, (e1 - e0) * C], U32, name="h_codes_%d" % e0 if g != 1 else "par_words_0", align_bytes=64)
             scales = keep.tile([P, (e1 - e0) * C], U8, name="h_scales_%d" % e0, align_bytes=64)
             nc.vector.quantize_mx(out=codes[:].bitcast(FP8X4), scales=scales[:],
                                   in_=h_tiles[g][:].rearrange("p s t -> p (s t)"))
@@ -196,12 +197,12 @@ def tile_moe_duo_relu2_kernel(
                 slot_lists = [load_list("slot_list%d" % r, p) for r, p in enumerate((pos1, pos2, pos3))]
                 gates = keep.tile([P, TOP, T], F32, name="gates")
                 nc.sync.dma_start(gates[:], gate.rearrange("r p t -> p r t"))
-                for r in range(2):
+                for r in range(TOP):
                     nc.sync.dma_start(gate_rows[4 * r : 4 * r + 4, :], gate[r, 0, :].rearrange("(b t) -> b t", b=4))
-            for late in {2: (0,), 4: (1, 2), 6: (3, 4), 8: (5, 6), 9: (7,), 10: (8,), 11: (9,)}.get(e, ()):
+            for late in {2: (0, 1), 4: (2, 3), 6: (4, 5), 8: (6, 7), 10: (8,), 11: (9,)}.get(e, ()):
                 turn(late)
                 square(late)
-            if e == 6:
+            if e == 5:
                 quantise(0)
         quantise(1)
         for e in (E - 2, E - 1):
@@ -234,24 +235,26 @@ def tile_moe_duo_relu2_kernel(
             for g in range(3):
                 second_layer(nb, 4 * g, 4 * g + 4, fills[nb][g], False)
 
-        def picked(nb, r):
-            return y[nb][:].indirect(slot_lists[r][:])
+        half = T // 2
 
-        def weighted_pick(nb, r):
-            part = keep.tile([P, T], F32, name="part%d" % (TOP * nb + r))
-            nc.vector.tensor_tensor(part[:], picked(nb, r), gates[:, r, :], ALU.mult)
+        def picked(nb, r, t0, t1):
+            return y[nb][:].indirect(slot_lists[r][:, t0 // 16 : t1 // 16])
+
+        def weighted_pick(nb, r, t0=0):
+            part = keep.tile([P, T - t0], F32, name="part%d" % (TOP * nb + r))
+            nc.vector.tensor_tensor(part[:], picked(nb, r, t0, T), gates[:, r, t0:T], ALU.mult)
             return part
 
-        def turn_and_add(b, parts):
-            acc = bank(b, [P, NB, P])
+        def turn_and_add(b, parts, blocks=range(NB)):
+            acc = bank(b, [P, len(blocks), P])
             for i, part in enumerate(parts):
-                for tb in range(NB):
-                    nc.tensor.matmul(acc[:, tb, :], part[:, tb * P : (tb + 1) * P], ident[:], is_transpose=True,
-                                     start=(i == 0 and tb == 0), stop=(i == len(parts) - 1 and tb == NB - 1))
+                for j, tb in enumerate(blocks):
+                    nc.tensor.matmul(acc[:, j, :], part[:, tb * P : (tb + 1) * P], ident[:], is_transpose=True,
+                                     start=(i == 0 and j == 0), stop=(i == len(parts) - 1 and j == len(blocks) - 1))
             return acc[:].rearrange("p b c -> p (b c)")
 
         def copied(acc):
-            t = ring.tile([P, T], F32, name="staged", bufs=8)
+            t = ring.tile([P, acc.shape[1]], F32, name="staged", bufs=8)
             nc.scalar.copy(t[:], acc)
             return t
 
@@ -260,43 +263,59 @@ def tile_moe_duo_relu2_kernel(
 
         gate_bank = bank(7, [P, P])
         nc.tensor.transpose(gate_bank[:], gate_rows[:], ident[:])
-        gate_cols = keep.tile([P, 8], F32, name="gate_cols")
-        nc.scalar.copy(gate_cols[:], gate_bank[:, 0:8])
+        gate_cols = keep.tile([P, TOP * NB], F32, name="gate_cols")
+        nc.scalar.copy(gate_cols[:], gate_bank[:, 0 : TOP * NB])
 
-        def plain_pick(r):
-            part = keep.tile([P, T], F32, name="plain%d" % r)
-            nc.scalar.activation(part[:], picked(3, r), ACT.Copy)
+        def plain_pick(r, t1=T):
+            part = keep.tile([P, t1], F32, name="plain%d" % r)
+            nc.scalar.activation(part[:], picked(3, r, 0, t1), ACT.Copy)
             return part
 
         def weighted_copy(acc, r):
-            t = keep.tile([P, T], F32, name="weighted%d" % r)
-            for tb in range(NB):
+            t = keep.tile([P, acc.shape[1]], F32, name="weighted%d" % r)
+            for tb in range(acc.shape[1] // P):
                 nc.scalar.activation(t[:, tb * P : (tb + 1) * P], acc[:, tb * P : (tb + 1) * P], ACT.Copy,
                                      scale=gate_cols[:, 4 * r + tb : 4 * r + tb + 1])
             return t
 
+        def add_turned(acc, part, first, start, stop):
+            count = acc.shape[1] // P
+            for j in range(count):
+                nc.tensor.matmul(acc[:, j * P : (j + 1) * P], part[:, (first + j) * P : (first + j + 1) * P], ident[:],
+                                 is_transpose=True, start=(start and j == 0), stop=(stop and j == count - 1))
+
         fill_block(1)
         parts = {(nb, r): weighted_pick(nb, r) for nb in range(2) for r in range(TOP)}
         fill_block(3)
-        turned0 = turn_and_add(5, [plain_pick(0)])
+        plain0 = plain_pick(0)
+        summed0 = turn_and_add(3, [parts[0, r] for r in range(TOP)])
+        turned0 = turn_and_add(5, [plain0])
         fill_block(2)
+        sum0 = copied(summed0)
+        parts[3, 2] = weighted_pick(3, 2, SPLIT)
         parts.update({(2, r): weighted_pick(2, r) for r in range(TOP)})
-        plain1 = plain_pick(1)
-        sum0 = copied(turn_and_add(0, [parts[0, r] for r in range(TOP)]))
-        parts[3, 2] = weighted_pick(3, 2)
-        sum1 = copied(turn_and_add(6, [parts[1, r] for r in range(TOP)]))
-        turned1 = turn_and_add(7, [plain1])
+        weighted = weighted_copy(turned0, 0)
+        sum1 = copied(turn_and_add(0, [parts[1, r] for r in range(TOP)]))
         store(0, copied(turn_and_add(1, [sum0])), 0, T)
-        weighted = [weighted_copy(turned0, 0)]
+        turned1 = turn_and_add(7, [plain_pick(1)])
         store(1, copied(turn_and_add(2, [sum1])), 0, T)
-        weighted.append(weighted_copy(turned1, 1))
+        turned2 = turn_and_add(6, [plain_pick(2, SPLIT)], range(SPLIT // P))
+        upper = bank(3, [P, T - SPLIT])
+        lower = bank(4, [P, SPLIT])
+        add_turned(upper, weighted, SPLIT // P, True, False)
+        add_turned(lower, weighted, 0, True, False)
+        weighted = weighted_copy(turned1, 1)
+        add_turned(upper, weighted, SPLIT // P, False, True)
+        add_turned(lower, weighted, 0, False, False)
+        add_turned(lower, weighted_copy(turned2, 2), 0, False, True)
         pair = keep.tile([P, T], F32, name="pair")
         nc.vector.tensor_tensor(pair[:], parts[2, 0][:], parts[2, 1][:], ALU.add)
-        back = {3: turn_and_add(3, weighted), 2: pair}
-        half = T // 2
-        for nb in (3, 2):
-            result = keep.tile([P, T], F32, name={3: "result3", 2: "weighted1"}[nb])
-            for t0 in (0, half):
-                nc.vector.tensor_tensor(result[:, t0 : t0 + half], back[nb][:, t0 : t0 + half],
-                                        parts[nb, 2][:, t0 : t0 + half], ALU.add)
-                store(nb, result, t0, t0 + half)
+        result = keep.tile([P, T - SPLIT], F32, name="result3")
+        nc.vector.tensor_tensor(result[:], upper[:], parts[3, 2][:], ALU.add)
+        nc.sync.dma_start(out[3 * P : 4 * P, SPLIT:T], result[:])
+        store(3, copied(lower[:]), 0, SPLIT)
+        result = keep.tile([P, T], F32, name="weighted1")
+        for t0 in (0, half):
+            nc.vector.tensor_tensor(result[:, t0 : t0 + half], pair[:, t0 : t0 + half],
+                                    parts[2, 2][:, t0 : t0 + half], ALU.add)
+            store(2, result, t0, t0 + half)

@@ -25,7 +25,7 @@ SCALE_GROUPS = (1, 2, 2, 2, 2, 2, 1)
 GATHER_SLOTS = {"words": 2, "scales": 2}
 LOAD_GROUPS = (2, 2, 2, 2, 2, 2)
 PLANE_GROUPS = (6, 6)
-SPLIT = 128
+SPLIT = 256
 QUANT_GROUPS = (4, 4, 3, 1)
 PRE_BANKS = (0, 1, 2, 0, 1, 2, 0, 1, 2, 0, 1, 2)
 TURN_BANKS = (3, 4, 5, 3, 4, 5, 3, 4, 5, 3, 4, 5)
@@ -197,8 +197,9 @@ def tile_moe_duo_relu2_kernel(
                 slot_lists = [load_list("slot_list%d" % r, p) for r, p in enumerate((pos1, pos2, pos3))]
                 gates = keep.tile([P, TOP, T], F32, name="gates")
                 nc.sync.dma_start(gates[:], gate.rearrange("r p t -> p r t"))
-                for r in range(TOP):
-                    nc.sync.dma_start(gate_rows[4 * r : 4 * r + 4, :], gate[r, 0, :].rearrange("(b t) -> b t", b=4))
+                for r, width in enumerate((T, T, SPLIT)):
+                    nc.sync.dma_start(gate_rows[4 * r : 4 * r + width // P, :],
+                                      gate[r, 0, 0:width].rearrange("(b t) -> b t", t=P))
             for late in {2: (0, 1), 4: (2, 3), 6: (4, 5), 8: (6, 7), 10: (8,), 11: (9,)}.get(e, ()):
                 turn(late)
                 square(late)
@@ -263,8 +264,8 @@ def tile_moe_duo_relu2_kernel(
 
         gate_bank = bank(7, [P, P])
         nc.tensor.transpose(gate_bank[:], gate_rows[:], ident[:])
-        gate_cols = keep.tile([P, TOP * NB], F32, name="gate_cols")
-        nc.scalar.copy(gate_cols[:], gate_bank[:, 0 : TOP * NB])
+        gate_cols = keep.tile([P, 2 * NB + SPLIT // P], F32, name="gate_cols")
+        nc.scalar.copy(gate_cols[:], gate_bank[:, 0 : 2 * NB + SPLIT // P])
 
         def plain_pick(r, t1=T):
             part = keep.tile([P, t1], F32, name="plain%d" % r)

@@ -227,9 +227,9 @@ def tile_moe_duo_relu2_kernel(
         quantise(2)
         second_layer(0, 0, 4, 0, True)
         quantise(3)
-        second_layer(0, 4, 8, 4, False)
-        second_layer(0, 8, 11, 3, True)
-        second_layer(0, 11, 12, 6, False)
+        second_layer(0, 4, 8, 7, False)
+        second_layer(0, 8, 11, 3, False)
+        second_layer(0, 11, 12, 6, True)
         fills = {1: (4, 3, 0), 3: (6, 4, 3), 2: (0, 6, 4)}
 
         def fill_block(nb):

@@ -192,11 +192,26 @@ def tile_moe_duo_relu2_kernel(
                     gather(sort, ends.index(e + 1) + GATHER_SLOTS[sort])
             if e == 3:
                 w2_plane = load_plane(early, w2_scales, 0, E)
-                w2_tile = keep.tile([P, E * 2 * N], U8, name="w2", align_bytes=64)
-                w2 = load_words(w2_tile[:], w2_words, 0, E)
                 slot_lists = [load_list("slot_list%d" % r, p) for r, p in enumerate((pos1, pos2, pos3))]
-                gates = keep.tile([P, TOP, T], F32, name="gates")
-                nc.sync.dma_start(gates[:], gate.rearrange("r p t -> p r t"))
+                w2 = []
+                gates = []
+
+                def load_w2_half(h):
+                    t = keep.tile([P, E * N], U8, name="w2_%d" % h, align_bytes=64)
+                    nc.sync.dma_start(t[:].rearrange("p (e b) -> p e b", b=N).bitcast(I32),
+                                      w2_words[:, 0, :, h * N : (h + 1) * N].rearrange("e p b -> p e b").bitcast(I32))
+                    w2.append(t)
+
+                def load_gate(r):
+                    t = keep.tile([P, T], F32, name="gate%d" % r)
+                    nc.sync.dma_start(t[:], gate[r])
+                    gates.append(t)
+
+                load_w2_half(0)
+                load_gate(0)
+                load_gate(1)
+                load_w2_half(1)
+                load_gate(2)
                 for r, width in enumerate((T, T, SPLIT)):
                     nc.sync.dma_start(gate_rows[4 * r : 4 * r + width // P, :],
                                       gate[r, 0, 0:width].rearrange("(b t) -> b t", t=P))
@@ -216,7 +231,7 @@ def tile_moe_duo_relu2_kernel(
             acc = bank(b, [P, (e1 - e0) * C])
             for e in range(e0, e1):
                 nc.tensor.matmul_mx(out=acc[:, (e - e0) * C : (e - e0 + 1) * C],
-                                    lhsT=w2[e][:, 2 * nb * P : 2 * (nb + 1) * P].bitcast(FP4X4),
+                                    lhsT=w2[nb // 2][:, e * N + 2 * (nb % 2) * P : e * N + 2 * (nb % 2 + 1) * P].bitcast(FP4X4),
                                     lhsT_scale=w2_plane[e][:, nb * P : (nb + 1) * P],
                                     rhs=h_codes[e].bitcast(FP8X4), rhs_scale=h_scales[e], start=True, stop=True)
             if on_vector:
@@ -243,7 +258,7 @@ def tile_moe_duo_relu2_kernel(
 
         def weighted_pick(nb, r, t0=0):
             part = keep.tile([P, T - t0], F32, name="part%d" % (TOP * nb + r))
-            nc.vector.tensor_tensor(part[:], picked(nb, r, t0, T), gates[:, r, t0:T], ALU.mult)
+            nc.vector.tensor_tensor(part[:], picked(nb, r, t0, T), gates[r][:, t0:T], ALU.mult)
             return part
 
         def turn_and_add(b, parts, blocks=range(NB)):

from contextlib import ExitStack

import concourse.mybir as mybir
from concourse.masks import make_identity

K, T, E, C, H, N, TOP = 512, 512, 12, 128, 512, 512, 3
S = E * C
FLOPS = 2 * S * (2 * K * H + H * N)

F32 = mybir.dt.float32
BF16 = mybir.dt.bfloat16
I32 = mybir.dt.int32
U32 = mybir.dt.uint32
U16 = mybir.dt.uint16
U8 = mybir.dt.uint8
FP8X4 = mybir.dt.float8_e4m3fn_x4
FP4X4 = mybir.dt.float4_e2m1fn_x4
ACT = mybir.ActivationFunctionType
ALU = mybir.AluOpType

P = 128
NB = N // P
WORD_GROUPS = (1, 2, 2, 2, 2, 2, 1)
SCALE_GROUPS = (1, 2, 2, 2, 2, 2, 1)
GATHER_SLOTS = {"words": 2, "scales": 2}
LOAD_GROUPS = (2, 2, 2, 2, 2, 2)
PLANE_GROUPS = (6, 6)
SPLIT = 256
QUANT_GROUPS = (4, 4, 3, 1)
PRE_BANKS = (0, 1, 2, 0, 1, 2, 0, 1, 2, 0, 1, 2)
TURN_BANKS = (3, 4, 5, 3, 4, 5, 3, 4, 5, 3, 4, 5)


def spans(sizes):
    return [(sum(sizes[:g]), sum(sizes[: g + 1])) for g in range(len(sizes))]


def tile_moe_duo_relu2_kernel(
    tc, x_words, x_scales, w1_words, w1_scales, wp_words, wp_scales, w2_words, w2_scales,
    gate, offs, pos1, pos2, pos3, offs2, out,
):
    nc = tc.nc
    with ExitStack() as ctx:
        keep = ctx.enter_context(tc.tile_pool(name="keep", bufs=1))
        ring = ctx.enter_context(tc.tile_pool(name="ring", bufs=3))
        psum = ctx.enter_context(tc.psum_pool(name="psum", bufs=1))

        def bank(b, shape):
            return psum.tile(shape, F32, name="bank%d" % b)

        def load_list(name, src):
            t = keep.tile([P, src.shape[1]], U16, name=name)
            nc.sync.dma_start(t[:], src)
            return t

        def zeroed_plane(name, shape, engine):
            t = keep.tile(shape, U8, name=name, align_bytes=64)
            engine.memset(t[:].bitcast(I32), 0)
            return t

        def load_plane(plane, src, e0, e1):
            rows = src[e0:e1, 0].rearrange("e (Q r) n -> r Q e n", r=4)
            for r in range(4):
                nc.sync.dma_start(plane[r:P:32, :].rearrange("p (e n) -> p e n", n=H).bitcast(I32), rows[r].bitcast(I32))
            return [plane[:, (e - e0) * H : (e - e0 + 1) * H] for e in range(e0, e1)]

        def load_words(t, src, e0, e1):
            nc.sync.dma_start(t.rearrange("p (e b) -> p e b", b=2 * H).bitcast(I32),
                              src[e0:e1, 0].rearrange("e p b -> p e b").bitcast(I32))
            return [t[:, (e - e0) * 2 * H : (e - e0 + 1) * 2 * H] for e in range(e0, e1)]

        (a0, a1), (b0, b1) = spans(PLANE_GROUPS)
        x_plane = zeroed_plane("x_plane", [P, T], nc.gpsimd)
        ident = keep.tile([P, P], F32, name="ident")
        make_identity(nc, ident[:])
        gate_rows = keep.tile([P, P], F32, name="gate_rows")
        nc.gpsimd.memset(gate_rows[:], 0.0)
        w1_plane_a = zeroed_plane("w1_plane_a", [P, (a1 - a0) * H], nc.vector)
        wp_plane_a = zeroed_plane("wp_plane_a", [P, (a1 - a0) * H], nc.vector)
        wp_plane_b = zeroed_plane("wp_plane_b", [P, (b1 - b0) * H], nc.vector)
        w1_plane_b = zeroed_plane("w1_plane_b", [P, (b1 - b0) * H], nc.gpsimd)


        early = keep.tile([P, E * N], U8, name="early", align_bytes=64)
        places = {("w1", 0): early[:, 0:2048], ("wp", 0): early[:, 2048:4096], ("wp", 1): early[:, 4096:6144]}
        w1 = []
        wp = []

        def load_group(name, g):
            e0, e1 = spans(LOAD_GROUPS)[g]
            if (name, g) not in places:
                t = keep.tile([P, (e1 - e0) * 2 * H], U8, name="%s_%d" % (name, g), align_bytes=64)
                places[name, g] = t[:]
            dst, src = {"w1": (w1, w1_words), "wp": (wp, wp_words)}[name]
            dst.extend(load_words(places[name, g], src, e0, e1))

        token_list = load_list("token_list", offs)
        x_table = keep.tile([P, T], U32, name="x_table")
        nc.sync.dma_start(x_table[:].bitcast(I32), x_words[0].rearrange("p t d -> p (t d)").bitcast(I32))
        partner_list = load_list("partner_list", offs2)
        x_rows = x_scales[0].rearrange("(Q r) t -> r Q t", r=4)
        for r in range(4):
            if r == 3:
                load_group("w1", 0)
                load_group("wp", 0)
            nc.sync.dma_start(x_plane[r:P:32, :].bitcast(I32), x_rows[r].bitcast(I32))
        w1_plane = load_plane(w1_plane_a, w1_scales, a0, a1)
        wp_plane = load_plane(wp_plane_a, wp_scales, a0, a1)
        for g in (1, 2):
            load_group("wp", g)
            load_group("w1", g)
        wp_plane.extend(load_plane(wp_plane_b, wp_scales, b0, b1))
        load_group("wp", 3)
        w1_plane.extend(load_plane(w1_plane_b, w1_scales, b0, b1))
        load_group("w1", 3)
        for g in (4, 5):
            load_group("wp", g)
            load_group("w1", g)

        gathered = {"words": [], "scales": []}
        sorts = {"words": (WORD_GROUPS, x_table, U32), "scales": (SCALE_GROUPS, x_plane, U8)}

        def gather(sort, g):
            groups, table, dtype = sorts[sort]
            e0, e1 = spans(groups)[g]
            cols = slice(e0 * C // 16, e1 * C // 16)
            pair = []
            for side, lst in (("tok", token_list), ("par", partner_list)):
                t = keep.tile([P, (e1 - e0) * C], dtype, name="%s_%s_%d" % (side, sort, g % GATHER_SLOTS[sort]), align_bytes=64)
                nc.vector.tensor_copy(t[:], table[:].indirect(lst[:, cols]))
                pair.append(t)
            for e in range(e0, e1):
                gathered[sort].append([t[:, (e - e0) * C : (e - e0 + 1) * C] for t in pair])

        for sort in ("words", "scales"):
            for g in range(GATHER_SLOTS[sort]):
                gather(sort, g)

        h_tiles = []
        h_view = []
        for e0, e1 in spans(QUANT_GROUPS):
            t = keep.tile([P, (e1 - e0) * C, 4], BF16, name="h_%d" % e0, align_bytes=64)
            h_tiles.append(t)
            h_view.extend(t[:, (e - e0) * C : (e - e0 + 1) * C, :] for e in range(e0, e1))

        relu = []

        def first_layer(e):
            tok_words, par_words = gathered["words"][e]
            tok_scales, par_scales = gathered["scales"][e]
            pre = bank(PRE_BANKS[e], [P, H])
            nc.tensor.matmul_mx(out=pre[:], lhsT=tok_words.bitcast(FP8X4), lhsT_scale=tok_scales,
                                rhs=w1[e].bitcast(FP4X4), rhs_scale=w1_plane[e], start=True, stop=False)
            nc.tensor.matmul_mx(out=pre[:], lhsT=par_words.bitcast(FP8X4), lhsT_scale=par_scales,
                                rhs=wp[e].bitcast(FP4X4), rhs_scale=wp_plane[e], start=False, stop=True)
            r = ring.tile([P, 4, P], F32, name="relu", bufs=4)
            stepped = pre[:].rearrange("s (q t) -> s t q", t=4)
            if e >= E - 2:
                nc.vector.tensor_scalar(r[:], stepped, 0.0, None, ALU.max)
            else:
                nc.scalar.activation(r[:], stepped, ACT.Relu)
            relu.append(r)

        turned = []

        def turn(e):
            tile = bank(TURN_BANKS[e], [P, 4, C])
            for t in range(4):
                nc.tensor.transpose(tile[:, t, :], relu[e][:, t, :], ident[:])
            turned.append(tile)

        def square(e):
            nc.scalar.activation(h_view[e], turned[e][:].rearrange("q t s -> q s t"), ACT.Square)

        h_codes = []
        h_scales = []

        def quantise(g):
            e0, e1 = spans(QUANT_GROUPS)[g]
            codes = keep.tile([P, (e1 - e0) * C], U32, name="h_codes_%d" % e0 if g != 1 else "par_words_0", align_bytes=64)
            scales = keep.tile([P, (e1 - e0) * C], U8, name="h_scales_%d" % e0, align_bytes=64)
            nc.vector.quantize_mx(out=codes[:].bitcast(FP8X4), scales=scales[:],
                                  in_=h_tiles[g][:].rearrange("p s t -> p (s t)"))
            h_codes.extend(codes[:, (e - e0) * C : (e - e0 + 1) * C] for e in range(e0, e1))
            h_scales.extend(scales[:, (e - e0) * C : (e - e0 + 1) * C] for e in range(e0, e1))

        for e in range(E):
            first_layer(e)
            for sort in ("words", "scales"):
                ends = [e1 for e0, e1 in spans(sorts[sort][0])]
                if e + 1 in ends[: len(ends) - GATHER_SLOTS[sort]]:
                    gather(sort, ends.index(e + 1) + GATHER_SLOTS[sort])
            if e == 3:
                w2_plane = load_plane(early, w2_scales, 0, E)
                slot_lists = [load_list("slot_list%d" % r, p) for r, p in enumerate((pos1, pos2, pos3))]
                w2 = []
                gates = []

                def load_w2_half(h):
                    t = keep.tile([P, E * N], U8, name="w2_%d" % h, align_bytes=64)
                    nc.sync.dma_start(t[:].rearrange("p (e b) -> p e b", b=N).bitcast(I32),
                                      w2_words[:, 0, :, h * N : (h + 1) * N].rearrange("e p b -> p e b").bitcast(I32))
                    w2.append(t)

                def load_gate(r):
                    t = keep.tile([P, T], F32, name="gate%d" % r)
                    nc.sync.dma_start(t[:], gate[r])
                    gates.append(t)

                load_w2_half(0)
                load_gate(0)
                load_gate(1)
                load_w2_half(1)
                load_gate(2)
                for r, width in enumerate((T, T, SPLIT)):
                    nc.sync.dma_start(gate_rows[4 * r : 4 * r + width // P, :],
                                      gate[r, 0, 0:width].rearrange("(b t) -> b t", t=P))
            for late in {2: (0, 1), 4: (2, 3), 6: (4, 5), 8: (6, 7), 10: (8,), 11: (9,)}.get(e, ()):
                turn(late)
                square(late)
            if e == 5:
                quantise(0)
        quantise(1)
        for e in (E - 2, E - 1):
            turn(e)
            square(e)

        y = [keep.tile([P, S], F32, name="y_%d" % nb) for nb in range(NB)]

        def second_layer(nb, e0, e1, b, on_vector):
            acc = bank(b, [P, (e1 - e0) * C])
            for e in range(e0, e1):
                nc.tensor.matmul_mx(out=acc[:, (e - e0) * C : (e - e0 + 1) * C],
                                    lhsT=w2[nb // 2][:, e * N + 2 * (nb % 2) * P : e * N + 2 * (nb % 2 + 1) * P].bitcast(FP4X4),
                                    lhsT_scale=w2_plane[e][:, nb * P : (nb + 1) * P],
                                    rhs=h_codes[e].bitcast(FP8X4), rhs_scale=h_scales[e], start=True, stop=True)
            if on_vector:
                nc.vector.tensor_copy(y[nb][:, e0 * C : e1 * C], acc[:])
            else:
                nc.scalar.copy(y[nb][:, e0 * C : e1 * C], acc[:])

        quantise(2)
        second_layer(0, 0, 4, 0, True)
        quantise(3)
        second_layer(0, 4, 8, 7, False)
        second_layer(0, 8, 11, 3, False)
        second_layer(0, 11, 12, 6, True)
        fills = {1: (4, 3, 0), 3: (6, 4, 3), 2: (0, 6, 4)}

        def fill_block(nb):
            for g in range(3):
                second_layer(nb, 4 * g, 4 * g + 4, fills[nb][g], False)

        half = T // 2

        def picked(nb, r, t0, t1):
            return y[nb][:].indirect(slot_lists[r][:, t0 // 16 : t1 // 16])

        def weighted_pick(nb, r, t0=0):
            part = keep.tile([P, T - t0], F32, name="part%d" % (TOP * nb + r))
            nc.vector.tensor_tensor(part[:], picked(nb, r, t0, T), gates[r][:, t0:T], ALU.mult)
            return part

        def turn_and_add(b, parts, blocks=range(NB)):
            acc = bank(b, [P, len(blocks), P])
            for i, part in enumerate(parts):
                for j, tb in enumerate(blocks):
                    nc.tensor.matmul(acc[:, j, :], part[:, tb * P : (tb + 1) * P], ident[:], is_transpose=True,
                                     start=(i == 0 and j == 0), stop=(i == len(parts) - 1 and j == len(blocks) - 1))
            return acc[:].rearrange("p b c -> p (b c)")

        def copied(acc):
            t = ring.tile([P, acc.shape[1]], F32, name="staged", bufs=8)
            nc.scalar.copy(t[:], acc)
            return t

        def store(nb, result, t0, t1):
            nc.sync.dma_start(out[nb * P : (nb + 1) * P, t0:t1], result[:, t0:t1])

        gate_bank = bank(7, [P, P])
        nc.tensor.transpose(gate_bank[:], gate_rows[:], ident[:])
        gate_cols = keep.tile([P, 2 * NB + SPLIT // P], F32, name="gate_cols")
        nc.scalar.copy(gate_cols[:], gate_bank[:, 0 : 2 * NB + SPLIT // P])

        def plain_pick(r, t1=T):
            part = keep.tile([P, t1], F32, name="plain%d" % r)
            nc.scalar.activation(part[:], picked(3, r, 0, t1), ACT.Copy)
            return part

        def weighted_copy(acc, r):
            t = keep.tile([P, acc.shape[1]], F32, name="weighted%d" % r)
            for tb in range(acc.shape[1] // P):
                nc.scalar.activation(t[:, tb * P : (tb + 1) * P], acc[:, tb * P : (tb + 1) * P], ACT.Copy,
                                     scale=gate_cols[:, 4 * r + tb : 4 * r + tb + 1])
            return t

        def add_turned(acc, part, first, start, stop):
            count = acc.shape[1] // P
            for j in range(count):
                nc.tensor.matmul(acc[:, j * P : (j + 1) * P], part[:, (first + j) * P : (first + j + 1) * P], ident[:],
                                 is_transpose=True, start=(start and j == 0), stop=(stop and j == count - 1))

        fill_block(1)
        parts = {(nb, r): weighted_pick(nb, r) for nb in range(2) for r in range(TOP)}
        fill_block(3)
        plain0 = plain_pick(0)
        summed0 = turn_and_add(3, [parts[0, r] for r in range(TOP)])
        turned0 = turn_and_add(5, [plain0])
        fill_block(2)
        sum0 = copied(summed0)
        parts[3, 2] = weighted_pick(3, 2, SPLIT)
        parts.update({(2, r): weighted_pick(2, r) for r in range(TOP)})
        weighted = weighted_copy(turned0, 0)
        sum1 = copied(turn_and_add(0, [parts[1, r] for r in range(TOP)]))
        store(0, copied(turn_and_add(1, [sum0])), 0, T)
        turned1 = turn_and_add(7, [plain_pick(1)])
        store(1, copied(turn_and_add(2, [sum1])), 0, T)
        turned2 = turn_and_add(6, [plain_pick(2, SPLIT)], range(SPLIT // P))
        upper = bank(3, [P, T - SPLIT])
        lower = bank(4, [P, SPLIT])
        add_turned(upper, weighted, SPLIT // P, True, False)
        add_turned(lower, weighted, 0, True, False)
        weighted = weighted_copy(turned1, 1)
        add_turned(upper, weighted, SPLIT // P, False, True)
        add_turned(lower, weighted, 0, False, False)
        add_turned(lower, weighted_copy(turned2, 2), 0, False, True)
        pair = keep.tile([P, T], F32, name="pair")
        nc.vector.tensor_tensor(pair[:], parts[2, 0][:], parts[2, 1][:], ALU.add)
        result = keep.tile([P, T - SPLIT], F32, name="result3")
        nc.vector.tensor_tensor(result[:], upper[:], parts[3, 2][:], ALU.add)
        nc.sync.dma_start(out[3 * P : 4 * P, SPLIT:T], result[:])
        store(3, copied(lower[:]), 0, SPLIT)
        result = keep.tile([P, T], F32, name="weighted1")
        for t0 in (0, half):
            nc.vector.tensor_tensor(result[:, t0 : t0 + half], pair[:, t0 : t0 + half],
                                    parts[2, 2][:, t0 : t0 + half], ALU.add)
            store(2, result, t0, t0 + half)
